import numpy as np
import ml_dtypes


def mxq(x, axis, fmt="e4m3"):
    dtype, down = {"e4m3": (ml_dtypes.float8_e4m3fn, 7), "e5m2": (ml_dtypes.float8_e5m2, 14)}[fmt]
    v = np.moveaxis(np.asarray(x, np.float32).astype(ml_dtypes.bfloat16).astype(np.float64), axis, -1)
    blocks = v.reshape(v.shape[:-1] + (-1, 32))
    amax = np.abs(blocks).max(-1, keepdims=True)
    byte = np.maximum(np.where(amax > 0, np.frexp(amax)[1] - 1 + 127, 0) - down, 1)
    scale = np.exp2(byte - 127.0)
    codes = (blocks / scale).astype(np.float32).astype(dtype).astype(np.float64)
    return np.moveaxis((codes * scale).reshape(v.shape), -1, axis)


WIDE = False


def mx_kscale(k):
    if not WIDE:
        return np.ones(k)
    levels = np.array([10, -10, 5, -5, 0])
    if k % 512:
        return np.exp2(np.random.permutation(np.resize(levels, k // 32))).repeat(32)
    a = np.empty((k // 512, 16))
    for p in range(k // 512):
        a[p, :8] = np.random.permutation(np.resize(levels, 8))
        for g in range(8):
            far = levels[np.abs(levels - a[p, g]) >= 10]
            a[p, g + 8] = far[np.random.randint(len(far))]
    return np.exp2(a.ravel()).repeat(32)


def f64(x):
    return np.asarray(x).astype(np.float64)


def striped(idx):
    return np.tile(idx.reshape(-1, 16).T, (8, 1)).astype(np.uint16)


def unstriped(offs):
    return offs[:16].T.reshape(-1).astype(np.int64)


def striped8(idx):
    return np.concatenate([x.reshape(-1, 16).T for x in idx]).astype(np.uint16)


def runs(offs, k):
    lists = np.stack([offs[16 * r : 16 * r + 16].T.reshape(-1) for r in range(8)]).astype(np.int64)
    return lists[np.arange(k) % 512 // 64]


def pack_weight(w):
    k, n = w.shape
    w = f64(np.asarray(w, np.float32).astype(ml_dtypes.bfloat16)).reshape(k // 32, 32, n)
    amax = np.abs(w).max(1)
    byte = np.clip(np.where(amax > 0, np.frexp(amax)[1] - 1 + 127 - 7, 1), 1, 254)
    scaled = (w * np.exp2(127.0 - byte)[:, None, :]).reshape(k, n).astype(np.float32)
    words = np.ascontiguousarray(scaled.reshape(k // 512, 128, 4, n).transpose(0, 1, 3, 2)).astype(ml_dtypes.float8_e4m3fn).view(np.uint8)
    return words, np.ascontiguousarray(byte.astype(np.uint8).reshape(k // 512, 16, n))


def unpack_weight(words, scales):
    g, p, n, _ = words.shape
    vals = np.ascontiguousarray(words).view(ml_dtypes.float8_e4m3fn).astype(np.float64) * np.repeat(np.exp2(scales.astype(np.float64) - 127.0), 8, axis=1)[..., None]
    return vals.transpose(0, 1, 3, 2).reshape(g * 512, n)


E2M1 = np.array([0.0, 0.5, 1.0, 1.5, 2.0, 3.0, 4.0, 6.0, -0.0, -0.5, -1.0, -1.5, -2.0, -3.0, -4.0, -6.0])


def pack_fp4(w):
    k, n = w.shape
    w = f64(np.asarray(w, np.float32).astype(ml_dtypes.bfloat16)).reshape(k // 32, 32, n)
    amax = np.abs(w).max(1)
    mant, ex = np.frexp(amax / 6.0)
    byte = np.clip(np.where(amax > 0, np.where(mant > 0.5, ex, ex - 1) + 127, 1), 1, 254)
    scaled = (w * np.exp2(127.0 - byte)[:, None, :]).reshape(k, n).astype(np.float32)
    c = np.ascontiguousarray(scaled.reshape(k // 512, 128, 4, n).transpose(0, 1, 3, 2)).astype(ml_dtypes.float4_e2m1fn).view(np.uint8) & 0xF
    words = (c[..., 0::2] | (c[..., 1::2] << 4)).reshape(k // 512, 128, 2 * n)
    return np.ascontiguousarray(words), np.ascontiguousarray(byte.astype(np.uint8).reshape(k // 512, 16, n))


def unpack_fp4(words, scales):
    g, _, n = scales.shape
    words = np.ascontiguousarray(words).reshape(g, 128, n, 2)
    nib = np.empty((g, 128, n, 4), np.uint8)
    nib[..., 0::2] = words & 0xF
    nib[..., 1::2] = words >> 4
    vals = E2M1[nib] * np.repeat(np.exp2(scales.astype(np.float64) - 127.0), 8, axis=1)[..., None]
    return vals.transpose(0, 1, 3, 2).reshape(g * 512, n)


def planes(y):
    n, m = y.shape
    v = y.astype(np.float32).astype(ml_dtypes.bfloat16).astype(np.float64).reshape(n // 32, 32, m)
    top = np.abs(v).max(1)
    byte = np.clip(np.where(top > 0, np.frexp(top)[1] - 1 + 127 - 7, 1), 1, 254)
    codes = (v * np.exp2(127.0 - byte)[:, None, :]).reshape(n, m).astype(np.float32).astype(ml_dtypes.float8_e4m3fn).view(np.uint8)
    words = codes.reshape(n // 512, 128, 4, m).transpose(0, 1, 3, 2)
    return np.ascontiguousarray(words), np.ascontiguousarray(byte.astype(np.uint8).reshape(n // 512, 16, m))


K, T, S, H, C = 512, 2048, 512, 512, 512


def setup_inputs():
    n = np.random.standard_normal
    s = mx_kscale(K)[:, None]
    packed_xT = pack_weight(n((K, T)) * s)
    packed_w1 = pack_fp4(n((K, H)) / np.sqrt(K) / s)
    packed_w2 = pack_fp4(n((K, H)) / np.sqrt(K) / s)
    return {
        "x_words": packed_xT[0],
        "x_scales": packed_xT[1],
        "w1_words": packed_w1[0],
        "w1_scales": packed_w1[1],
        "w2_words": packed_w2[0],
        "w2_scales": packed_w2[1],
        "gs": (np.random.uniform(0.5, 1.5, (K, 1)) / s).astype(np.float32),
        "offs": striped(np.random.permutation(T)[:S]),
        "two": striped(np.random.permutation(T)[:S]),
        "n1": striped8(np.stack([np.random.permutation(S) for _ in range(8)])),
        "n2": striped8(np.stack([np.random.permutation(S) for _ in range(8)])),
        "cand": striped(np.random.permutation(T)[:C]),
        "n3": striped8(np.stack([np.random.permutation(S) for _ in range(8)])),
        "n4": striped8(np.stack([np.random.permutation(S) for _ in range(8)])),
    }


def reference(x_words, x_scales, w1_words, w1_scales, w2_words, w2_scales, gs, offs, two, n1, n2, cand, n3, n4):
    x_cand = unpack_weight(x_words, x_scales)[:, unstriped(cand)]
    xq = unpack_weight(x_words, x_scales)[:, unstriped(offs)]
    y = unpack_fp4(w1_words, w1_scales).T @ xq
    x_two = unpack_weight(x_words, x_scales)[:, unstriped(two)]
    d = unpack_fp4(w2_words, w2_scales).T @ x_two
    z = f64(gs) * (0.75 * (y * (d[np.arange(H)[:, None], runs(n2, H)]) - ((y[np.arange(H)[:, None], runs(n1, H)]) * d)))
    s = 0.0625 * ((x_cand.T @ mxq(z, 0, "e4m3")))
    pa = s[np.arange(C)[:, None], runs(n3, C)]
    kr = np.exp(-0.5 * ((s - pa) ** 2))
    pb = s[np.arange(C)[:, None], runs(n4, C)]
    kr2 = np.exp(-0.5 * ((s - pb) ** 2))
    out_0 = (kr * pa + kr2 * pb) / (kr + kr2 + 0.5)
    return (out_0,) + planes(out_0)

@@ -1,0 +1,207 @@
+from contextlib import ExitStack
+
+import concourse.mybir as mybir
+
+F32 = mybir.dt.float32
+BF16 = mybir.dt.bfloat16
+I32 = mybir.dt.int32
+U32 = mybir.dt.uint32
+U16 = mybir.dt.uint16
+U8 = mybir.dt.uint8
+FP8X4 = mybir.dt.float8_e4m3fn_x4
+FP4X4 = mybir.dt.float4_e2m1fn_x4
+ACT = mybir.ActivationFunctionType
+ALU = mybir.AluOpType
+
+P = 128
+PACK = 4
+T = 2048
+S = 512
+HALF = S // 2
+WINDOW = 2 * S
+FLOPS = 3 * 2 * 512 * 512 * 512
+
+
+def tile_picked_twccrossbkern_none_po_kernel(
+    tc, x_words, x_scales, w1_words, w1_scales, w2_words, w2_scales, gs, offs, two, n1, n2, cand, n3, n4, out_0, out_1, out_2
+):
+    nc = tc.nc
+    with ExitStack() as ctx:
+        pool = ctx.enter_context(tc.tile_pool(name="keep", bufs=1))
+        psum = ctx.enter_context(tc.psum_pool(name="psum", bufs=1))
+
+        def sbuf(name, shape, dtype):
+            return pool.tile(shape, dtype, name=name, align_bytes=64)
+
+        def load_list(name, source):
+            tile = pool.tile([P, S // 16], U16, name=name)
+            nc.sync.dma_start(tile[:], source)
+            return tile
+
+        def load_scale_rows(plane, source):
+            for q in range(4):
+                nc.sync.dma_start(plane[32 * q : 32 * q + 4, :].bitcast(I32), source[0, 4 * q : 4 * q + 4, :].bitcast(I32))
+
+        xs = sbuf("xs", [P, T], U8)
+        ws_raw = [sbuf("ws_raw%d" % a, [P, S], U8) for a in range(2)]
+        nc.vector.memset(xs[:].bitcast(I32), 0)
+        for a in range(2):
+            nc.vector.memset(ws_raw[a][:].bitcast(I32), 0)
+
+        ww_raw = []
+        for a, words in enumerate((w1_words, w2_words)):
+            raw = sbuf("ww_raw%d" % a, [P, 2 * S], U8)
+            nc.sync.dma_start(raw[:].bitcast(I32), words[0].bitcast(I32))
+            ww_raw.append(raw)
+        offs_t = load_list("offs_t", offs)
+        two_t = load_list("two_t", two)
+        load_scale_rows(xs, x_scales)
+        cand_t = load_list("cand_t", cand)
+        for a, scales in enumerate((w1_scales, w2_scales)):
+            load_scale_rows(ws_raw[a], scales)
+        gain = sbuf("gain", [P, PACK], F32)
+        nc.sync.dma_start(gain[:], gs.rearrange("(p t) o -> p (t o)", t=PACK))
+        xw = sbuf("xw", [P, T], I32)
+        nc.sync.dma_start(xw[:], x_words[0].rearrange("p n t -> p (n t)").bitcast(I32))
+        n2_t = load_list("n2_t", n2)
+        n1_t = load_list("n1_t", n1)
+        n3_t = load_list("n3_t", n3)
+        n4_t = load_list("n4_t", n4)
+
+        def pick_scales(name, offsets):
+            tile = sbuf(name, [P, S], U8)
+            nc.vector.tensor_copy(tile[:], xs[:].indirect(offsets[:]))
+            return tile
+
+        def pick_words(name, offsets):
+            tile = sbuf(name, [P, S], U32)
+            nc.vector.tensor_copy(tile[:], xw[:].bitcast(U32).indirect(offsets[:]))
+            return tile
+
+        def deal_bytes(name, source, width):
+            tile = sbuf(name, [P, S * width], U8)
+            nc.vector.tensor_copy(
+                tile[:].rearrange("p (t m b) -> p t m b", t=PACK, b=width),
+                source[:].rearrange("p (m t b) -> p t m b", t=PACK, b=width),
+            )
+            return tile
+
+        ww = [deal_bytes("ww%d" % a, ww_raw[a], 2) for a in range(2)]
+        offs_s = pick_scales("offs_s", offs_t)
+        two_s = pick_scales("two_s", two_t)
+        ws = [deal_bytes("ws%d" % a, ws_raw[a], 1) for a in range(2)]
+        offs_w = pick_words("offs_w", offs_t)
+        two_w = pick_words("two_w", two_t)
+        cand_s_raw = pick_scales("cand_s_raw", cand_t)
+        cand_w_raw = pick_words("cand_w_raw", cand_t)
+        cand_s = deal_bytes("cand_s", cand_s_raw, 1)
+        cand_w = sbuf("cand_w", [P, S], I32)
+        nc.vector.tensor_copy(
+            cand_w[:].rearrange("p (t m) -> p t m", t=PACK),
+            cand_w_raw[:].bitcast(I32).rearrange("p (m t) -> p t m", t=PACK),
+        )
+
+        banks = [psum.tile([P, S], F32, name="bank%d" % b) for b in range(8)]
+        y_win = [sbuf("y_win%d" % t, [P, WINDOW], F32) for t in range(PACK)]
+        d_win = [sbuf("d_win%d" % t, [P, WINDOW], F32) for t in range(PACK)]
+        s_win = [sbuf("s_win%d" % t, [P, WINDOW], F32) for t in range(PACK)]
+        left = sbuf("left", [P, PACK, S], F32)
+        right = sbuf("right", [P, PACK, S], F32)
+
+        def project(bank, a, t, words, scales):
+            nc.tensor.matmul_mx(
+                bank[:],
+                lhsT=ww[a][:, 2 * P * t : 2 * P * (t + 1)].bitcast(FP4X4),
+                lhsT_scale=ws[a][:, P * t : P * (t + 1)],
+                rhs=words[:].bitcast(FP8X4),
+                rhs_scale=scales[:],
+                start=True,
+                stop=True,
+            )
+
+        for t in range(PACK):
+            project(banks[t], 0, t, offs_w, offs_s)
+            project(banks[PACK + t], 1, t, two_w, two_s)
+            nc.scalar.activation(y_win[t][:, :S], banks[t][:], ACT.Copy, scale=gain[:, t : t + 1])
+            nc.scalar.activation(d_win[t][:, :S], banks[PACK + t][:], ACT.Copy, scale=0.75)
+        for t in range(PACK):
+            nc.vector.tensor_tensor(left[:, t, :], d_win[t][:].indirect(n2_t[:]), y_win[t][:, :S], ALU.mult)
+            nc.vector.tensor_tensor(right[:, t, :], y_win[t][:].indirect(n1_t[:]), d_win[t][:, :S], ALU.mult)
+
+        z_bf = sbuf("z_bf", [P, PACK * S], BF16)
+        z_w = sbuf("z_w", [P, S], U32)
+        z_s = sbuf("z_s", [P, S], U8)
+        halves = [slice(h * HALF, (h + 1) * HALF) for h in range(2)]
+        wide = [slice(h * HALF * PACK, (h + 1) * HALF * PACK) for h in range(2)]
+        for h in range(2):
+            nc.vector.tensor_tensor(
+                z_bf[:, wide[h]].rearrange("p (c i t) -> p c t i", i=4, t=PACK),
+                left[:, :, halves[h]].rearrange("p t (c i) -> p c t i", i=4),
+                right[:, :, halves[h]].rearrange("p t (c i) -> p c t i", i=4),
+                ALU.subtract,
+            )
+        for h in range(2):
+            nc.vector.quantize_mx(z_w[:, halves[h]].bitcast(FP8X4), z_s[:, halves[h]], z_bf[:, wide[h]])
+        for t in range(PACK):
+            for h in range(2):
+                nc.tensor.matmul_mx(
+                    banks[t][:, halves[h]],
+                    lhsT=cand_w[:, P * t : P * (t + 1)].bitcast(FP8X4),
+                    lhsT_scale=cand_s[:, P * t : P * (t + 1)],
+                    rhs=z_w[:, halves[h]].bitcast(FP8X4),
+                    rhs_scale=z_s[:, halves[h]],
+                    start=True,
+                    stop=True,
+                )
+
+        picked = [sbuf("picked%d" % t, [P, 2, S], F32) for t in range(PACK)]
+        diff = [sbuf("diff%d" % t, [P, 2, S], F32) for t in range(PACK)]
+        square = [sbuf("square%d" % t, [P, 2, S], F32) for t in range(PACK)]
+        terms = [sbuf("terms%d" % t, [P, 2, 2, S], F32) for t in range(PACK)]
+        sums = [sbuf("sums%d" % t, [P, 2, S], F32) for t in range(PACK)]
+        den2 = [sbuf("den2_%d" % t, [P, S], F32) for t in range(PACK)]
+        result = sbuf("result", [P, PACK, S], F32)
+
+        def look_up(t):
+            nc.scalar.activation(s_win[t][:, :S], banks[t][:], ACT.Copy, scale=0.0625)
+            nc.vector.tensor_copy(picked[t][:, 0, :], s_win[t][:].indirect(n3_t[:]))
+            nc.vector.tensor_copy(picked[t][:, 1, :], s_win[t][:].indirect(n4_t[:]))
+            nc.vector.scalar_tensor_tensor(
+                diff[t][:], banks[t][:].unsqueeze(1).to_broadcast([P, 2, S]), 0.0625, picked[t][:], ALU.mult, ALU.subtract
+            )
+            nc.scalar.activation(square[t][:], diff[t][:], ACT.Square)
+            nc.scalar.activation(terms[t][:, :, 0, :], square[t][:], ACT.Exp, scale=-0.5)
+
+        def combine(t):
+            nc.vector.tensor_tensor(terms[t][:, :, 1, :], terms[t][:, :, 0, :], picked[t][:], ALU.mult)
+            nc.vector.tensor_tensor(sums[t][:], terms[t][:, 0, :, :], terms[t][:, 1, :, :], ALU.add)
+            nc.scalar.activation(den2[t][:], sums[t][:, 0, :], ACT.Square, bias=0.5)
+
+        for t in range(PACK):
+            look_up(t)
+            if t > 0:
+                combine(t - 1)
+        combine(PACK - 1)
+
+        inverse = [square[PACK - 1][:, 0, :], square[PACK - 1][:, 1, :], den2[0][:], den2[1][:]]
+        rows = out_0.rearrange("(p t) j -> p t j", t=PACK)
+        for t in range(PACK):
+            nc.scalar.activation(inverse[t], den2[t][:], ACT.Abs_reciprocal_sqrt)
+            nc.vector.tensor_tensor(result[:, t, :], sums[t][:, 1, :], inverse[t], ALU.mult)
+            nc.sync.dma_start(rows[:, t, :], result[:, t, :])
+
+        o_bf = sbuf("o_bf", [P, PACK * S], BF16)
+        o_w = sbuf("o_w", [P, S], I32)
+        o_s = sbuf("o_s", [P, S], U8)
+        words_out = out_1[0].rearrange("p n t -> p (n t)").bitcast(I32)
+        for h in range(2):
+            nc.vector.tensor_copy(
+                o_bf[:, wide[h]].rearrange("p (c i t) -> p c t i", i=4, t=PACK),
+                result[:, :, halves[h]].rearrange("p t (c i) -> p c t i", i=4),
+            )
+        for h in range(2):
+            nc.vector.quantize_mx(o_w[:, halves[h]].bitcast(FP8X4), o_s[:, halves[h]], o_bf[:, wide[h]])
+            nc.sync.dma_start(words_out[:, halves[h]], o_w[:, halves[h]])
+        for q in range(4):
+            engine = nc.scalar if q % 2 else nc.sync
+            engine.dma_start(out_2[0, 4 * q : 4 * q + 4, :].bitcast(I32), o_s[32 * q : 32 * q + 4, :].bitcast(I32))

@@ -19,6 +19,7 @@ T = 2048
 S = 512
 HALF = S // 2
 WINDOW = 2 * S
+GPSIMD_TILES = 2
 FLOPS = 3 * 2 * 512 * 512 * 512
 
 
@@ -44,25 +45,24 @@ def tile_picked_twccrossbkern_none_po_kernel(
 
         xs = sbuf("xs", [P, T], U8)
         ws_raw = [sbuf("ws_raw%d" % a, [P, S], U8) for a in range(2)]
-        nc.vector.memset(xs[:].bitcast(I32), 0)
+        nc.gpsimd.memset(xs[:, : T // 2].bitcast(I32), 0)
+        nc.vector.memset(xs[:, T // 2 :].bitcast(I32), 0)
         for a in range(2):
             nc.vector.memset(ws_raw[a][:].bitcast(I32), 0)
 
-        ww_raw = []
-        for a, words in enumerate((w1_words, w2_words)):
-            raw = sbuf("ww_raw%d" % a, [P, 2 * S], U8)
-            nc.sync.dma_start(raw[:].bitcast(I32), words[0].bitcast(I32))
-            ww_raw.append(raw)
         offs_t = load_list("offs_t", offs)
         two_t = load_list("two_t", two)
+        ww_raw = [sbuf("ww_raw%d" % a, [P, 2 * S], U8) for a in range(2)]
+        nc.sync.dma_start(ww_raw[0][:].bitcast(I32), w1_words[0].bitcast(I32))
+        gain = sbuf("gain", [P, PACK], F32)
+        nc.gpsimd.dma_start(gain[:], gs.rearrange("(p t) o -> p (t o)", t=PACK))
         load_scale_rows(xs, x_scales)
+        xw = sbuf("xw", [P, T], I32)
+        nc.sync.dma_start(xw[:], x_words[0].rearrange("p n t -> p (n t)").bitcast(I32))
+        nc.sync.dma_start(ww_raw[1][:].bitcast(I32), w2_words[0].bitcast(I32))
         cand_t = load_list("cand_t", cand)
         for a, scales in enumerate((w1_scales, w2_scales)):
             load_scale_rows(ws_raw[a], scales)
-        gain = sbuf("gain", [P, PACK], F32)
-        nc.sync.dma_start(gain[:], gs.rearrange("(p t) o -> p (t o)", t=PACK))
-        xw = sbuf("xw", [P, T], I32)
-        nc.sync.dma_start(xw[:], x_words[0].rearrange("p n t -> p (n t)").bitcast(I32))
         n2_t = load_list("n2_t", n2)
         n1_t = load_list("n1_t", n1)
         n3_t = load_list("n3_t", n3)
@@ -78,23 +78,25 @@ def tile_picked_twccrossbkern_none_po_kernel(
             nc.vector.tensor_copy(tile[:], xw[:].bitcast(U32).indirect(offsets[:]))
             return tile
 
-        def deal_bytes(name, source, width):
+        def deal_bytes(engine, name, source, width):
             tile = sbuf(name, [P, S * width], U8)
-            nc.vector.tensor_copy(
+            engine.tensor_copy(
                 tile[:].rearrange("p (t m b) -> p t m b", t=PACK, b=width),
                 source[:].rearrange("p (m t b) -> p t m b", t=PACK, b=width),
             )
             return tile
 
-        ww = [deal_bytes("ww%d" % a, ww_raw[a], 2) for a in range(2)]
+        ww, ws = [], []
+        for a in range(2):
+            ww.append(deal_bytes(nc.gpsimd, "ww%d" % a, ww_raw[a], 2))
+            ws.append(deal_bytes(nc.gpsimd, "ws%d" % a, ws_raw[a], 1))
         offs_s = pick_scales("offs_s", offs_t)
         two_s = pick_scales("two_s", two_t)
-        ws = [deal_bytes("ws%d" % a, ws_raw[a], 1) for a in range(2)]
         offs_w = pick_words("offs_w", offs_t)
         two_w = pick_words("two_w", two_t)
         cand_s_raw = pick_scales("cand_s_raw", cand_t)
         cand_w_raw = pick_words("cand_w_raw", cand_t)
-        cand_s = deal_bytes("cand_s", cand_s_raw, 1)
+        cand_s = deal_bytes(nc.vector, "cand_s", cand_s_raw, 1)
         cand_w = sbuf("cand_w", [P, S], I32)
         nc.vector.tensor_copy(
             cand_w[:].rearrange("p (t m) -> p t m", t=PACK),
@@ -104,7 +106,7 @@ def tile_picked_twccrossbkern_none_po_kernel(
         banks = [psum.tile([P, S], F32, name="bank%d" % b) for b in range(8)]
         y_win = [sbuf("y_win%d" % t, [P, WINDOW], F32) for t in range(PACK)]
         d_win = [sbuf("d_win%d" % t, [P, WINDOW], F32) for t in range(PACK)]
-        s_win = [sbuf("s_win%d" % t, [P, WINDOW], F32) for t in range(PACK)]
+        s_win = [sbuf("s_win%d" % t, [P, S], F32) for t in range(PACK)]
         left = sbuf("left", [P, PACK, S], F32)
         right = sbuf("right", [P, PACK, S], F32)
 
@@ -120,88 +122,130 @@ def tile_picked_twccrossbkern_none_po_kernel(
             )
 
         for t in range(PACK):
-            project(banks[t], 0, t, offs_w, offs_s)
-            project(banks[PACK + t], 1, t, two_w, two_s)
-            nc.scalar.activation(y_win[t][:, :S], banks[t][:], ACT.Copy, scale=gain[:, t : t + 1])
-            nc.scalar.activation(d_win[t][:, :S], banks[PACK + t][:], ACT.Copy, scale=0.75)
+            y_bank, d_bank = banks[PACK + t % 2], banks[PACK + 2 + t % 2]
+            project(y_bank, 0, t, offs_w, offs_s)
+            nc.scalar.activation(y_win[t][:, :S], y_bank[:], ACT.Copy, scale=gain[:, t : t + 1])
+            project(d_bank, 1, t, two_w, two_s)
+            nc.scalar.activation(d_win[t][:, :S], d_bank[:], ACT.Copy, scale=0.75)
+        last = PACK - 1
+        halves = [slice(0, HALF), slice(HALF, S)]
+
+        def entries(offsets, cols):
+            return offsets[:, cols.start // 16 : cols.stop // 16]
+
         for t in range(PACK):
-            nc.vector.tensor_tensor(left[:, t, :], d_win[t][:].indirect(n2_t[:]), y_win[t][:, :S], ALU.mult)
-            nc.vector.tensor_tensor(right[:, t, :], y_win[t][:].indirect(n1_t[:]), d_win[t][:, :S], ALU.mult)
+            for cols in halves if t == last else [slice(0, S)]:
+                nc.vector.tensor_tensor(left[:, t, cols], d_win[t][:].indirect(entries(n2_t, cols)), y_win[t][:, cols], ALU.mult)
+                nc.vector.tensor_tensor(right[:, t, cols], y_win[t][:].indirect(entries(n1_t, cols)), d_win[t][:, cols], ALU.mult)
 
         z_bf = sbuf("z_bf", [P, PACK * S], BF16)
         z_w = sbuf("z_w", [P, S], U32)
         z_s = sbuf("z_s", [P, S], U8)
-        halves = [slice(h * HALF, (h + 1) * HALF) for h in range(2)]
-        wide = [slice(h * HALF * PACK, (h + 1) * HALF * PACK) for h in range(2)]
-        for h in range(2):
-            nc.vector.tensor_tensor(
-                z_bf[:, wide[h]].rearrange("p (c i t) -> p c t i", i=4, t=PACK),
-                left[:, :, halves[h]].rearrange("p t (c i) -> p c t i", i=4),
-                right[:, :, halves[h]].rearrange("p t (c i) -> p c t i", i=4),
-                ALU.subtract,
-            )
-        for h in range(2):
-            nc.vector.quantize_mx(z_w[:, halves[h]].bitcast(FP8X4), z_s[:, halves[h]], z_bf[:, wide[h]])
-        for t in range(PACK):
-            for h in range(2):
-                nc.tensor.matmul_mx(
-                    banks[t][:, halves[h]],
-                    lhsT=cand_w[:, P * t : P * (t + 1)].bitcast(FP8X4),
-                    lhsT_scale=cand_s[:, P * t : P * (t + 1)],
-                    rhs=z_w[:, halves[h]].bitcast(FP8X4),
-                    rhs_scale=z_s[:, halves[h]],
-                    start=True,
-                    stop=True,
-                )
 
-        picked = [sbuf("picked%d" % t, [P, 2, S], F32) for t in range(PACK)]
-        diff = [sbuf("diff%d" % t, [P, 2, S], F32) for t in range(PACK)]
-        square = [sbuf("square%d" % t, [P, 2, S], F32) for t in range(PACK)]
+        def wide(cols):
+            return slice(cols.start * PACK, cols.stop * PACK)
+
+        def weave(tile, cols):
+            return tile[:, wide(cols)].rearrange("p (c i t) -> p c t i", i=4, t=PACK)
+
+        def planes(tile, cols):
+            return tile[:, :, cols].rearrange("p t (c i) -> p c t i", i=4)
+
+        def subtract(cols):
+            nc.vector.tensor_tensor(weave(z_bf, cols), planes(left, cols), planes(right, cols), ALU.subtract)
+
+        def quantize(words, scales, source, cols):
+            nc.vector.quantize_mx(words[:, cols].bitcast(FP8X4), scales[:, cols], source[:, wide(cols)])
+
+        def score(t, cols):
+            nc.tensor.matmul_mx(
+                banks[t][:, cols],
+                lhsT=cand_w[:, P * t : P * (t + 1)].bitcast(FP8X4),
+                lhsT_scale=cand_s[:, P * t : P * (t + 1)],
+                rhs=z_w[:, cols].bitcast(FP8X4),
+                rhs_scale=z_s[:, cols],
+                start=True,
+                stop=True,
+            )
+
+        def scale_scores(t, cols):
+            nc.scalar.activation(s_win[t][:, cols], banks[t][:, cols], ACT.Copy, scale=0.0625)
+
+        pieces = [slice(0, 256), slice(256, 384), slice(384, 512)]
+        subtract(pieces[0])
+        for i, cols in enumerate(pieces):
+            if i + 1 < len(pieces):
+                subtract(pieces[i + 1])
+            quantize(z_w, z_s, z_bf, cols)
+            score(0, cols)
+            scale_scores(0, cols)
+        for t in range(1, PACK):
+            score(t, slice(0, S))
+        scale_scores(1, slice(0, S))
+
+        quarters = [slice(P * b, P * (b + 1)) for b in range(4)]
+        units = [(t, cols) for t in range(PACK) for cols in halves]
+        units = [(0, cols) for cols in quarters[:2]] + units[1:-1] + [(last, cols) for cols in quarters[2:]]
         terms = [sbuf("terms%d" % t, [P, 2, 2, S], F32) for t in range(PACK)]
+        spare = sbuf("spare", [P, 2, S], F32)
+        square = sbuf("square", [P, PACK, 2, S], F32)
         sums = [sbuf("sums%d" % t, [P, 2, S], F32) for t in range(PACK)]
         den2 = [sbuf("den2_%d" % t, [P, S], F32) for t in range(PACK)]
         result = sbuf("result", [P, PACK, S], F32)
+        places = [terms[t][:, :, 1, cols] for t, cols in units]
+        loans = places[2:-2] + [terms[last][:, :, 1, halves[1]]] + [spare[:, :, cols] for t, cols in units if t == last]
 
-        def look_up(t):
-            nc.scalar.activation(s_win[t][:, :S], banks[t][:], ACT.Copy, scale=0.0625)
-            nc.vector.tensor_copy(picked[t][:, 0, :], s_win[t][:].indirect(n3_t[:]))
-            nc.vector.tensor_copy(picked[t][:, 1, :], s_win[t][:].indirect(n4_t[:]))
-            nc.vector.scalar_tensor_tensor(
-                diff[t][:], banks[t][:].unsqueeze(1).to_broadcast([P, 2, S]), 0.0625, picked[t][:], ALU.mult, ALU.subtract
-            )
-            nc.scalar.activation(square[t][:], diff[t][:], ACT.Square)
-            nc.scalar.activation(terms[t][:, :, 0, :], square[t][:], ACT.Exp, scale=-0.5)
+        for u, (t, cols) in enumerate(units):
+            width = cols.stop - cols.start
+            diff = loans[u][:, :, :width]
+            nc.vector.tensor_copy(terms[t][:, 0, 1, cols], s_win[t][:].indirect(entries(n3_t, cols)))
+            nc.vector.tensor_copy(terms[t][:, 1, 1, cols], s_win[t][:].indirect(entries(n4_t, cols)))
+            for a in range(2):
+                nc.vector.scalar_tensor_tensor(diff[:, a, :], banks[t][:, cols], 0.0625, places[u][:, a, :], ALU.mult, ALU.subtract)
+            if u < 2:
+                squared = s_win[2 + u][:, : 2 * width].rearrange("p (a j) -> p a j", a=2)
+            else:
+                squared = square[:, t, :, cols]
+            nc.scalar.activation(squared, diff, ACT.Square)
+            nc.scalar.activation(terms[t][:, :, 0, cols], squared, ACT.Exp, scale=-0.5)
+            if u < 2:
+                scale_scores(2 + u, slice(0, S))
 
-        def combine(t):
-            nc.vector.tensor_tensor(terms[t][:, :, 1, :], terms[t][:, :, 0, :], picked[t][:], ALU.mult)
-            nc.vector.tensor_tensor(sums[t][:], terms[t][:, 0, :, :], terms[t][:, 1, :, :], ALU.add)
+        def weigh(engine, t, cols):
+            engine.tensor_tensor(terms[t][:, :, 1, cols], terms[t][:, :, 0, cols], terms[t][:, :, 1, cols], ALU.mult)
+
+        def add(engine, t, kinds, cols):
+            engine.tensor_tensor(sums[t][:, kinds, cols], terms[t][:, 0, kinds, cols], terms[t][:, 1, kinds, cols], ALU.add)
+
+        for t in range(PACK):
+            engine = nc.gpsimd if t < GPSIMD_TILES else nc.vector
+            spans = [cols for tile, cols in units if tile == t] if t < GPSIMD_TILES else [slice(0, S)]
+            for cols in spans:
+                if t < GPSIMD_TILES - 1 or cols.stop < S:
+                    weigh(engine, t, cols)
+                    add(engine, t, slice(0, 2), cols)
+                else:
+                    add(engine, t, slice(0, 1), cols)
+                    weigh(engine, t, cols)
+                    add(nc.vector, t, slice(1, 2), cols)
             nc.scalar.activation(den2[t][:], sums[t][:, 0, :], ACT.Square, bias=0.5)
 
-        for t in range(PACK):
-            look_up(t)
-            if t > 0:
-                combine(t - 1)
-        combine(PACK - 1)
-
-        inverse = [square[PACK - 1][:, 0, :], square[PACK - 1][:, 1, :], den2[0][:], den2[1][:]]
+        inverse = [square[:, last, 0, :], den2[0][:], den2[1][:], den2[2][:]]
         rows = out_0.rearrange("(p t) j -> p t j", t=PACK)
-        for t in range(PACK):
-            nc.scalar.activation(inverse[t], den2[t][:], ACT.Abs_reciprocal_sqrt)
-            nc.vector.tensor_tensor(result[:, t, :], sums[t][:, 1, :], inverse[t], ALU.mult)
-            nc.sync.dma_start(rows[:, t, :], result[:, t, :])
-
         o_bf = sbuf("o_bf", [P, PACK * S], BF16)
         o_w = sbuf("o_w", [P, S], I32)
         o_s = sbuf("o_s", [P, S], U8)
         words_out = out_1[0].rearrange("p n t -> p (n t)").bitcast(I32)
-        for h in range(2):
-            nc.vector.tensor_copy(
-                o_bf[:, wide[h]].rearrange("p (c i t) -> p c t i", i=4, t=PACK),
-                result[:, :, halves[h]].rearrange("p t (c i) -> p c t i", i=4),
-            )
-        for h in range(2):
-            nc.vector.quantize_mx(o_w[:, halves[h]].bitcast(FP8X4), o_s[:, halves[h]], o_bf[:, wide[h]])
-            nc.sync.dma_start(words_out[:, halves[h]], o_w[:, halves[h]])
+        for t in range(PACK):
+            nc.scalar.activation(inverse[t], den2[t][:], ACT.Abs_reciprocal_sqrt)
+            for cols in halves if t == last else [slice(0, S)]:
+                nc.vector.tensor_tensor(result[:, t, cols], sums[t][:, 1, cols], inverse[t][:, cols], ALU.mult)
+            nc.sync.dma_start(rows[:, t, :], result[:, t, :])
+        nc.scalar.copy(weave(o_bf, halves[0]), planes(result, halves[0]))
+        nc.vector.tensor_copy(weave(o_bf, halves[1]), planes(result, halves[1]))
+        for cols in reversed(halves):
+            quantize(o_w, o_s, o_bf, cols)
+            nc.sync.dma_start(words_out[:, cols], o_w[:, cols])
         for q in range(4):
             engine = nc.scalar if q % 2 else nc.sync
             engine.dma_start(out_2[0, 4 * q : 4 * q + 4, :].bitcast(I32), o_s[32 * q : 32 * q + 4, :].bitcast(I32))

@@ -54,12 +54,12 @@ def tile_picked_twccrossbkern_none_po_kernel(
         two_t = load_list("two_t", two)
         ww_raw = [sbuf("ww_raw%d" % a, [P, 2 * S], U8) for a in range(2)]
         nc.sync.dma_start(ww_raw[0][:].bitcast(I32), w1_words[0].bitcast(I32))
+        nc.gpsimd.dma_start(ww_raw[1][:].bitcast(I32), w2_words[0].bitcast(I32))
         gain = sbuf("gain", [P, PACK], F32)
         nc.gpsimd.dma_start(gain[:], gs.rearrange("(p t) o -> p (t o)", t=PACK))
         load_scale_rows(xs, x_scales)
         xw = sbuf("xw", [P, T], I32)
         nc.sync.dma_start(xw[:], x_words[0].rearrange("p n t -> p (n t)").bitcast(I32))
-        nc.sync.dma_start(ww_raw[1][:].bitcast(I32), w2_words[0].bitcast(I32))
         cand_t = load_list("cand_t", cand)
         for a, scales in enumerate((w1_scales, w2_scales)):
             load_scale_rows(ws_raw[a], scales)
@@ -87,8 +87,8 @@ def tile_picked_twccrossbkern_none_po_kernel(
             return tile
 
         ww, ws = [], []
-        for a in range(2):
-            ww.append(deal_bytes(nc.gpsimd, "ww%d" % a, ww_raw[a], 2))
+        for a, engine in enumerate((nc.vector, nc.gpsimd)):
+            ww.append(deal_bytes(engine, "ww%d" % a, ww_raw[a], 2))
             ws.append(deal_bytes(nc.gpsimd, "ws%d" % a, ws_raw[a], 1))
         offs_s = pick_scales("offs_s", offs_t)
         two_s = pick_scales("two_s", two_t)
@@ -193,7 +193,8 @@ def tile_picked_twccrossbkern_none_po_kernel(
         den2 = [sbuf("den2_%d" % t, [P, S], F32) for t in range(PACK)]
         result = sbuf("result", [P, PACK, S], F32)
         places = [terms[t][:, :, 1, cols] for t, cols in units]
-        loans = places[2:-2] + [terms[last][:, :, 1, halves[1]]] + [spare[:, :, cols] for t, cols in units if t == last]
+        loans = places[2:-2] + [terms[last][:, :, 1, halves[1]]] + [spare[:, :, cols] for t, cols in units[-3:-1]]
+        loans.append(sums[GPSIMD_TILES - 1][:, 1, halves[1]].rearrange("p (a j) -> p a j", a=2))
 
         for u, (t, cols) in enumerate(units):
             width = cols.stop - cols.start
@@ -224,11 +225,17 @@ def tile_picked_twccrossbkern_none_po_kernel(
                 if t < GPSIMD_TILES - 1 or cols.stop < S:
                     weigh(engine, t, cols)
                     add(engine, t, slice(0, 2), cols)
+                elif t == last:
+                    nc.vector.scalar_tensor_tensor(sums[t][:, 0, :], terms[t][:, 0, 0, :], 0.5, terms[t][:, 1, 0, :], ALU.add, ALU.add)
+                    weigh(engine, t, cols)
+                    nc.vector.tensor_tensor(den2[t][:], sums[t][:, 0, :], sums[t][:, 0, :], ALU.mult)
+                    add(nc.vector, t, slice(1, 2), cols)
                 else:
                     add(engine, t, slice(0, 1), cols)
                     weigh(engine, t, cols)
                     add(nc.vector, t, slice(1, 2), cols)
-            nc.scalar.activation(den2[t][:], sums[t][:, 0, :], ACT.Square, bias=0.5)
+            if t < last:
+                nc.scalar.activation(den2[t][:], sums[t][:, 0, :], ACT.Square, bias=0.5)
 
         inverse = [square[:, last, 0, :], den2[0][:], den2[1][:], den2[2][:]]
         rows = out_0.rearrange("(p t) j -> p t j", t=PACK)

from contextlib import ExitStack

import concourse.mybir as mybir

F32 = mybir.dt.float32
BF16 = mybir.dt.bfloat16
I32 = mybir.dt.int32
U32 = mybir.dt.uint32
U16 = mybir.dt.uint16
U8 = mybir.dt.uint8
FP8X4 = mybir.dt.float8_e4m3fn_x4
FP4X4 = mybir.dt.float4_e2m1fn_x4
ACT = mybir.ActivationFunctionType
ALU = mybir.AluOpType

P = 128
PACK = 4
T = 2048
S = 512
HALF = S // 2
WINDOW = 2 * S
GPSIMD_TILES = 2
FLOPS = 3 * 2 * 512 * 512 * 512


def tile_picked_twccrossbkern_none_po_kernel(
    tc, x_words, x_scales, w1_words, w1_scales, w2_words, w2_scales, gs, offs, two, n1, n2, cand, n3, n4, out_0, out_1, out_2
):
    nc = tc.nc
    with ExitStack() as ctx:
        pool = ctx.enter_context(tc.tile_pool(name="keep", bufs=1))
        psum = ctx.enter_context(tc.psum_pool(name="psum", bufs=1))

        def sbuf(name, shape, dtype):
            return pool.tile(shape, dtype, name=name, align_bytes=64)

        def load_list(name, source):
            tile = pool.tile([P, S // 16], U16, name=name)
            nc.sync.dma_start(tile[:], source)
            return tile

        def load_scale_rows(plane, source):
            for q in range(4):
                nc.sync.dma_start(plane[32 * q : 32 * q + 4, :].bitcast(I32), source[0, 4 * q : 4 * q + 4, :].bitcast(I32))

        xs = sbuf("xs", [P, T], U8)
        ws_raw = [sbuf("ws_raw%d" % a, [P, S], U8) for a in range(2)]
        nc.gpsimd.memset(xs[:, : T // 2].bitcast(I32), 0)
        nc.vector.memset(xs[:, T // 2 :].bitcast(I32), 0)
        for a in range(2):
            nc.vector.memset(ws_raw[a][:].bitcast(I32), 0)

        offs_t = load_list("offs_t", offs)
        two_t = load_list("two_t", two)
        ww_raw = [sbuf("ww_raw%d" % a, [P, 2 * S], U8) for a in range(2)]
        nc.sync.dma_start(ww_raw[0][:].bitcast(I32), w1_words[0].bitcast(I32))
        nc.gpsimd.dma_start(ww_raw[1][:].bitcast(I32), w2_words[0].bitcast(I32))
        gain = sbuf("gain", [P, PACK], F32)
        nc.gpsimd.dma_start(gain[:], gs.rearrange("(p t) o -> p (t o)", t=PACK))
        load_scale_rows(xs, x_scales)
        xw = sbuf("xw", [P, T], I32)
        nc.sync.dma_start(xw[:], x_words[0].rearrange("p n t -> p (n t)").bitcast(I32))
        cand_t = load_list("cand_t", cand)
        for a, scales in enumerate((w1_scales, w2_scales)):
            load_scale_rows(ws_raw[a], scales)
        n2_t = load_list("n2_t", n2)
        n1_t = load_list("n1_t", n1)
        n3_t = load_list("n3_t", n3)
        n4_t = load_list("n4_t", n4)

        def pick_scales(name, offsets):
            tile = sbuf(name, [P, S], U8)
            nc.vector.tensor_copy(tile[:], xs[:].indirect(offsets[:]))
            return tile

        def pick_words(name, offsets):
            tile = sbuf(name, [P, S], U32)
            nc.vector.tensor_copy(tile[:], xw[:].bitcast(U32).indirect(offsets[:]))
            return tile

        def deal_bytes(engine, name, source, width):
            tile = sbuf(name, [P, S * width], U8)
            engine.tensor_copy(
                tile[:].rearrange("p (t m b) -> p t m b", t=PACK, b=width),
                source[:].rearrange("p (m t b) -> p t m b", t=PACK, b=width),
            )
            return tile

        ww, ws = [], []
        for a, engine in enumerate((nc.vector, nc.gpsimd)):
            ww.append(deal_bytes(engine, "ww%d" % a, ww_raw[a], 2))
            ws.append(deal_bytes(nc.gpsimd, "ws%d" % a, ws_raw[a], 1))
        offs_s = pick_scales("offs_s", offs_t)
        two_s = pick_scales("two_s", two_t)
        offs_w = pick_words("offs_w", offs_t)
        two_w = pick_words("two_w", two_t)
        cand_s_raw = pick_scales("cand_s_raw", cand_t)
        cand_w_raw = pick_words("cand_w_raw", cand_t)
        cand_s = deal_bytes(nc.vector, "cand_s", cand_s_raw, 1)
        cand_w = sbuf("cand_w", [P, S], I32)
        nc.vector.tensor_copy(
            cand_w[:].rearrange("p (t m) -> p t m", t=PACK),
            cand_w_raw[:].bitcast(I32).rearrange("p (m t) -> p t m", t=PACK),
        )

        banks = [psum.tile([P, S], F32, name="bank%d" % b) for b in range(8)]
        y_win = [sbuf("y_win%d" % t, [P, WINDOW], F32) for t in range(PACK)]
        d_win = [sbuf("d_win%d" % t, [P, WINDOW], F32) for t in range(PACK)]
        s_win = [sbuf("s_win%d" % t, [P, S], F32) for t in range(PACK)]
        left = sbuf("left", [P, PACK, S], F32)
        right = sbuf("right", [P, PACK, S], F32)

        def project(bank, a, t, words, scales):
            nc.tensor.matmul_mx(
                bank[:],
                lhsT=ww[a][:, 2 * P * t : 2 * P * (t + 1)].bitcast(FP4X4),
                lhsT_scale=ws[a][:, P * t : P * (t + 1)],
                rhs=words[:].bitcast(FP8X4),
                rhs_scale=scales[:],
                start=True,
                stop=True,
            )

        for t in range(PACK):
            y_bank, d_bank = banks[PACK + t % 2], banks[PACK + 2 + t % 2]
            project(y_bank, 0, t, offs_w, offs_s)
            nc.scalar.activation(y_win[t][:, :S], y_bank[:], ACT.Copy, scale=gain[:, t : t + 1])
            project(d_bank, 1, t, two_w, two_s)
            nc.scalar.activation(d_win[t][:, :S], d_bank[:], ACT.Copy, scale=0.75)
        last = PACK - 1
        halves = [slice(0, HALF), slice(HALF, S)]

        def entries(offsets, cols):
            return offsets[:, cols.start // 16 : cols.stop // 16]

        for t in range(PACK):
            for cols in halves if t == last else [slice(0, S)]:
                nc.vector.tensor_tensor(left[:, t, cols], d_win[t][:].indirect(entries(n2_t, cols)), y_win[t][:, cols], ALU.mult)
                nc.vector.tensor_tensor(right[:, t, cols], y_win[t][:].indirect(entries(n1_t, cols)), d_win[t][:, cols], ALU.mult)

        z_bf = sbuf("z_bf", [P, PACK * S], BF16)
        z_w = sbuf("z_w", [P, S], U32)
        z_s = sbuf("z_s", [P, S], U8)

        def wide(cols):
            return slice(cols.start * PACK, cols.stop * PACK)

        def weave(tile, cols):
            return tile[:, wide(cols)].rearrange("p (c i t) -> p c t i", i=4, t=PACK)

        def planes(tile, cols):
            return tile[:, :, cols].rearrange("p t (c i) -> p c t i", i=4)

        def subtract(cols):
            nc.vector.tensor_tensor(weave(z_bf, cols), planes(left, cols), planes(right, cols), ALU.subtract)

        def quantize(words, scales, source, cols):
            nc.vector.quantize_mx(words[:, cols].bitcast(FP8X4), scales[:, cols], source[:, wide(cols)])

        def score(t, cols):
            nc.tensor.matmul_mx(
                banks[t][:, cols],
                lhsT=cand_w[:, P * t : P * (t + 1)].bitcast(FP8X4),
                lhsT_scale=cand_s[:, P * t : P * (t + 1)],
                rhs=z_w[:, cols].bitcast(FP8X4),
                rhs_scale=z_s[:, cols],
                start=True,
                stop=True,
            )

        def scale_scores(t, cols):
            nc.scalar.activation(s_win[t][:, cols], banks[t][:, cols], ACT.Copy, scale=0.0625)

        pieces = [slice(0, 256), slice(256, 384), slice(384, 512)]
        subtract(pieces[0])
        for i, cols in enumerate(pieces):
            if i + 1 < len(pieces):
                subtract(pieces[i + 1])
            quantize(z_w, z_s, z_bf, cols)
            score(0, cols)
            scale_scores(0, cols)
        for t in range(1, PACK):
            score(t, slice(0, S))
        scale_scores(1, slice(0, S))

        quarters = [slice(P * b, P * (b + 1)) for b in range(4)]
        units = [(t, cols) for t in range(PACK) for cols in halves]
        units = [(0, cols) for cols in quarters[:2]] + units[1:-1] + [(last, cols) for cols in quarters[2:]]
        terms = [sbuf("terms%d" % t, [P, 2, 2, S], F32) for t in range(PACK)]
        spare = sbuf("spare", [P, 2, S], F32)
        square = sbuf("square", [P, PACK, 2, S], F32)
        sums = [sbuf("sums%d" % t, [P, 2, S], F32) for t in range(PACK)]
        den2 = [sbuf("den2_%d" % t, [P, S], F32) for t in range(PACK)]
        result = sbuf("result", [P, PACK, S], F32)
        places = [terms[t][:, :, 1, cols] for t, cols in units]
        loans = places[2:-2] + [terms[last][:, :, 1, halves[1]]] + [spare[:, :, cols] for t, cols in units[-3:-1]]
        loans.append(sums[GPSIMD_TILES - 1][:, 1, halves[1]].rearrange("p (a j) -> p a j", a=2))

        for u, (t, cols) in enumerate(units):
            width = cols.stop - cols.start
            diff = loans[u][:, :, :width]
            nc.vector.tensor_copy(terms[t][:, 0, 1, cols], s_win[t][:].indirect(entries(n3_t, cols)))
            nc.vector.tensor_copy(terms[t][:, 1, 1, cols], s_win[t][:].indirect(entries(n4_t, cols)))
            for a in range(2):
                nc.vector.scalar_tensor_tensor(diff[:, a, :], banks[t][:, cols], 0.0625, places[u][:, a, :], ALU.mult, ALU.subtract)
            if u < 2:
                squared = s_win[2 + u][:, : 2 * width].rearrange("p (a j) -> p a j", a=2)
            else:
                squared = square[:, t, :, cols]
            nc.scalar.activation(squared, diff, ACT.Square)
            nc.scalar.activation(terms[t][:, :, 0, cols], squared, ACT.Exp, scale=-0.5)
            if u < 2:
                scale_scores(2 + u, slice(0, S))

        def weigh(engine, t, cols):
            engine.tensor_tensor(terms[t][:, :, 1, cols], terms[t][:, :, 0, cols], terms[t][:, :, 1, cols], ALU.mult)

        def add(engine, t, kinds, cols):
            engine.tensor_tensor(sums[t][:, kinds, cols], terms[t][:, 0, kinds, cols], terms[t][:, 1, kinds, cols], ALU.add)

        for t in range(PACK):
            engine = nc.gpsimd if t < GPSIMD_TILES else nc.vector
            spans = [cols for tile, cols in units if tile == t] if t < GPSIMD_TILES else [slice(0, S)]
            for cols in spans:
                if t < GPSIMD_TILES - 1 or cols.stop < S:
                    weigh(engine, t, cols)
                    add(engine, t, slice(0, 2), cols)
                elif t == last:
                    nc.vector.scalar_tensor_tensor(sums[t][:, 0, :], terms[t][:, 0, 0, :], 0.5, terms[t][:, 1, 0, :], ALU.add, ALU.add)
                    weigh(engine, t, cols)
                    nc.vector.tensor_tensor(den2[t][:], sums[t][:, 0, :], sums[t][:, 0, :], ALU.mult)
                    add(nc.vector, t, slice(1, 2), cols)
                else:
                    add(engine, t, slice(0, 1), cols)
                    weigh(engine, t, cols)
                    add(nc.vector, t, slice(1, 2), cols)
            if t < last:
                nc.scalar.activation(den2[t][:], sums[t][:, 0, :], ACT.Square, bias=0.5)

        inverse = [square[:, last, 0, :], den2[0][:], den2[1][:], den2[2][:]]
        rows = out_0.rearrange("(p t) j -> p t j", t=PACK)
        o_bf = sbuf("o_bf", [P, PACK * S], BF16)
        o_w = sbuf("o_w", [P, S], I32)
        o_s = sbuf("o_s", [P, S], U8)
        words_out = out_1[0].rearrange("p n t -> p (n t)").bitcast(I32)
        for t in range(PACK):
            nc.scalar.activation(inverse[t], den2[t][:], ACT.Abs_reciprocal_sqrt)
            for cols in halves if t == last else [slice(0, S)]:
                nc.vector.tensor_tensor(result[:, t, cols], sums[t][:, 1, cols], inverse[t][:, cols], ALU.mult)
            nc.sync.dma_start(rows[:, t, :], result[:, t, :])
        nc.scalar.copy(weave(o_bf, halves[0]), planes(result, halves[0]))
        nc.vector.tensor_copy(weave(o_bf, halves[1]), planes(result, halves[1]))
        for cols in reversed(halves):
            quantize(o_w, o_s, o_bf, cols)
            nc.sync.dma_start(words_out[:, cols], o_w[:, cols])
        for q in range(4):
            engine = nc.scalar if q % 2 else nc.sync
            engine.dma_start(out_2[0, 4 * q : 4 * q + 4, :].bitcast(I32), o_s[32 * q : 32 * q + 4, :].bitcast(I32))
